import numpy as np
CORES = [18,19,22,23,26,27,30,31,98,99,102,103,106,107,110,111]
N = 16
H = 2
ROWS, COLS = 4, 4
PERIODIC = True
def setup_inputs(rng):
    return {"x": rng.standard_normal((N, 128, 128), dtype=np.float32)}
def reference(x):
    W = x.shape[2]
    y = np.zeros((N, 4, 128, H), x.dtype)
    for r in range(N):
        i, j = divmod(r, COLS)
        for k, (di, dj, cols) in enumerate([(-1, 0, slice(W - H, W)), (1, 0, slice(0, H)), (0, -1, slice(W - H, W)), (0, 1, slice(0, H))]):
            a, b = i + di, j + dj
            if PERIODIC:
                a, b = a % ROWS, b % COLS
            if 0 <= a < ROWS and 0 <= b < COLS:
                y[r][k] = x[a * COLS + b][:, cols]
    return {"y": y}

@@ -1,0 +1,48 @@
+from concourse.bass import DstId, RemoteDMATransfer
+
+H = 2
+ROWS, COLS = 4, 4
+
+SCRATCH = {
+    "first": ("dram", [128, H], "float32"),
+    "last": ("dram", [128, H], "float32"),
+    "land": ("dram", [4, 128, H], "float32"),
+}
+SEMAPHORES = ["loaded", "sent", "arrived", "stored"]
+
+ENG = 2
+
+
+def rank_program(g, core, T, topo):
+    rank = T.rank_of(core)
+    if rank is None:
+        return
+    i, j = divmod(rank, COLS)
+    W = T.x.shape[1]
+
+    def at(a, b):
+        return T.cores[(a % ROWS) * COLS + (b % COLS)]
+
+    g.sync.dma_start(T.first[:], T.x[:, 0:H]).then_inc(T.sem.loaded, 16)
+    g.scalar.dma_start(T.last[:], T.x[:, W - H:W]).then_inc(T.sem.loaded, 16)
+
+    north, south, west, east = at(i - 1, j), at(i + 1, j), at(i, j - 1), at(i, j + 1)
+    off_chip = [(north, T.first, 1), (south, T.last, 0)]
+    on_chip = [(west, T.first, 3), (east, T.last, 2)]
+    plan = []
+    for k, w in enumerate(off_chip):
+        plan.append((w, 0x0003 << (2 * k)))
+    for k, w in enumerate(on_chip):
+        plan.append((w, 0x0300 << (2 * k)))
+    transfers = []
+    for (dst, src, slot), m in plan:
+        rid, pid, _se = topo.addr(dst)
+        transfers.append(RemoteDMATransfer(dst_ids=[DstId(rid=rid, pnc=pid)], dma_engine_mask=m,
+                                           remote_sem=T.sem.arrived, src=src[:], dst=T.land[slot]))
+    g.wait_ge(T.sem.loaded, 32)
+    g.remote_dma_fused(transfers, local_sem=T.sem.sent)
+
+    g.sync.wait_ge(T.sem.arrived, 4 * ENG)
+    g.sync.dma_start(T.y[:], T.land[:]).then_inc(T.sem.stored, 16)
+    g.sync.wait_ge(T.sem.stored, 16)
+    g.wait_ge(T.sem.sent, 4 * ENG)

@@ -8,7 +8,7 @@ SCRATCH = {
     "last": ("dram", [128, H], "float32"),
     "land": ("dram", [4, 128, H], "float32"),
 }
-SEMAPHORES = ["loaded", "sent", "arrived", "stored"]
+SEMAPHORES = ["ld_far", "ld_near", "sent", "arrived", "stored"]
 
 ENG = 2
 
@@ -23,23 +23,29 @@ def rank_program(g, core, T, topo):
     def at(a, b):
         return T.cores[(a % ROWS) * COLS + (b % COLS)]
 
-    g.sync.dma_start(T.first[:], T.x[:, 0:H]).then_inc(T.sem.loaded, 16)
-    g.scalar.dma_start(T.last[:], T.x[:, W - H:W]).then_inc(T.sem.loaded, 16)
-
     north, south, west, east = at(i - 1, j), at(i + 1, j), at(i, j - 1), at(i, j + 1)
-    off_chip = [(north, T.first, 1), (south, T.last, 0)]
-    on_chip = [(west, T.first, 3), (east, T.last, 2)]
-    plan = []
-    for k, w in enumerate(off_chip):
-        plan.append((w, 0x0003 << (2 * k)))
-    for k, w in enumerate(on_chip):
-        plan.append((w, 0x0300 << (2 * k)))
+    up = (north, T.first, 1)
+    down = (south, T.last, 0)
+    left = (west, T.first, 3)
+    right = (east, T.last, 2)
+    far_is_up = not topo.mates(topo.chip(core), topo.chip(north))
+    far, near = (up, down) if far_is_up else (down, up)
+
+    cols = {"first": T.x[:, 0:H], "last": T.x[:, W - H:W]}
+    far_name, near_name = ("first", "last") if far_is_up else ("last", "first")
+    g.sync.dma_start(T[far_name][:], cols[far_name]).then_inc(T.sem.ld_far, 16)
+    g.scalar.dma_start(T[near_name][:], cols[near_name]).then_inc(T.sem.ld_near, 16)
+
+    rid, pid, _se = topo.addr(far[0])
+    g.wait_ge(T.sem.ld_far, 16)
+    g.remote_dma(T.land[far[2]], far[1][:], T.sem.arrived, T.sem.sent, pid, rid, 0x0003)
+
     transfers = []
-    for (dst, src, slot), m in plan:
+    for (dst, src, slot), m in ((near, 0x000C), (left, 0x0300), (right, 0x0C00)):
         rid, pid, _se = topo.addr(dst)
         transfers.append(RemoteDMATransfer(dst_ids=[DstId(rid=rid, pnc=pid)], dma_engine_mask=m,
                                            remote_sem=T.sem.arrived, src=src[:], dst=T.land[slot]))
-    g.wait_ge(T.sem.loaded, 32)
+    g.wait_ge(T.sem.ld_near, 16)
     g.remote_dma_fused(transfers, local_sem=T.sem.sent)
 
     g.sync.wait_ge(T.sem.arrived, 4 * ENG)

from concourse.bass import DstId, RemoteDMATransfer

H = 2
ROWS, COLS = 4, 4

SCRATCH = {
    "first": ("dram", [128, H], "float32"),
    "last": ("dram", [128, H], "float32"),
    "land": ("dram", [4, 128, H], "float32"),
}
SEMAPHORES = ["ld_far", "ld_near", "sent", "arrived", "stored"]

ENG = 2


def rank_program(g, core, T, topo):
    rank = T.rank_of(core)
    if rank is None:
        return
    i, j = divmod(rank, COLS)
    W = T.x.shape[1]

    def at(a, b):
        return T.cores[(a % ROWS) * COLS + (b % COLS)]

    north, south, west, east = at(i - 1, j), at(i + 1, j), at(i, j - 1), at(i, j + 1)
    up = (north, T.first, 1)
    down = (south, T.last, 0)
    left = (west, T.first, 3)
    right = (east, T.last, 2)
    far_is_up = not topo.mates(topo.chip(core), topo.chip(north))
    far, near = (up, down) if far_is_up else (down, up)

    cols = {"first": T.x[:, 0:H], "last": T.x[:, W - H:W]}
    far_name, near_name = ("first", "last") if far_is_up else ("last", "first")
    g.sync.dma_start(T[far_name][:], cols[far_name]).then_inc(T.sem.ld_far, 16)
    g.scalar.dma_start(T[near_name][:], cols[near_name]).then_inc(T.sem.ld_near, 16)

    rid, pid, _se = topo.addr(far[0])
    g.wait_ge(T.sem.ld_far, 16)
    g.remote_dma(T.land[far[2]], far[1][:], T.sem.arrived, T.sem.sent, pid, rid, 0x0003)

    transfers = []
    for (dst, src, slot), m in ((near, 0x000C), (left, 0x0300), (right, 0x0C00)):
        rid, pid, _se = topo.addr(dst)
        transfers.append(RemoteDMATransfer(dst_ids=[DstId(rid=rid, pnc=pid)], dma_engine_mask=m,
                                           remote_sem=T.sem.arrived, src=src[:], dst=T.land[slot]))
    g.wait_ge(T.sem.ld_near, 16)
    g.remote_dma_fused(transfers, local_sem=T.sem.sent)

    g.sync.wait_ge(T.sem.arrived, 4 * ENG)
    g.sync.dma_start(T.y[:], T.land[:]).then_inc(T.sem.stored, 16)
    g.sync.wait_ge(T.sem.stored, 16)
    g.wait_ge(T.sem.sent, 4 * ENG)
